import numpy as np
import ml_dtypes


def mxq(x, axis, fmt="e4m3"):
    dtype, down = {"e4m3": (ml_dtypes.float8_e4m3fn, 7), "e5m2": (ml_dtypes.float8_e5m2, 14)}[fmt]
    v = np.moveaxis(np.asarray(x, np.float32).astype(ml_dtypes.bfloat16).astype(np.float64), axis, -1)
    blocks = v.reshape(v.shape[:-1] + (-1, 32))
    amax = np.abs(blocks).max(-1, keepdims=True)
    byte = np.maximum(np.where(amax > 0, np.frexp(amax)[1] - 1 + 127, 0) - down, 1)
    scale = np.exp2(byte - 127.0)
    codes = (blocks / scale).astype(np.float32).astype(dtype).astype(np.float64)
    return np.moveaxis((codes * scale).reshape(v.shape), -1, axis)


WIDE = False


def mx_kscale(k):
    if not WIDE:
        return np.ones(k)
    levels = np.array([10, -10, 5, -5, 0])
    if k % 512:
        return np.exp2(np.random.permutation(np.resize(levels, k // 32))).repeat(32)
    a = np.empty((k // 512, 16))
    for p in range(k // 512):
        a[p, :8] = np.random.permutation(np.resize(levels, 8))
        for g in range(8):
            far = levels[np.abs(levels - a[p, g]) >= 10]
            a[p, g + 8] = far[np.random.randint(len(far))]
    return np.exp2(a.ravel()).repeat(32)


def f64(x):
    return np.asarray(x).astype(np.float64)


def striped(idx):
    return np.tile(np.asarray(idx).reshape(-1, 16).T, (8, 1)).astype(np.uint16)


def unstriped(offs):
    return offs[:16].T.reshape(-1).astype(np.int64)


E2M1 = np.array([0.0, 0.5, 1.0, 1.5, 2.0, 3.0, 4.0, 6.0, -0.0, -0.5, -1.0, -1.5, -2.0, -3.0, -4.0, -6.0])


def pack_weight(w, fmt):
    k, n = w.shape
    w = f64(np.asarray(w, np.float32).astype(ml_dtypes.bfloat16)).reshape(k // 32, 32, n)
    amax = np.abs(w).max(1)
    if fmt == "e4m3":
        byte = np.frexp(amax)[1] - 1 + 127 - 7
    else:
        mant, ex = np.frexp(amax / 6.0)
        byte = np.where(mant > 0.5, ex, ex - 1) + 127
    byte = np.clip(np.where(amax > 0, byte, 1), 1, 254)
    scaled = (w * np.exp2(127.0 - byte)[:, None, :]).reshape(k, n).astype(np.float32)
    by_word = np.ascontiguousarray(scaled.reshape(k // 512, 128, 4, n).transpose(0, 1, 3, 2))
    if fmt == "e4m3":
        words = by_word.astype(ml_dtypes.float8_e4m3fn).view(np.uint8)
    else:
        c = by_word.astype(ml_dtypes.float4_e2m1fn).view(np.uint8) & 0xF
        words = (c[..., 0::2] | (c[..., 1::2] << 4)).reshape(k // 512, 128, 2 * n)
    return np.ascontiguousarray(words), np.ascontiguousarray(byte.astype(np.uint8).reshape(k // 512, 16, n))


def unpack_weight(words, scales, fmt):
    g, _, n = scales.shape
    words = np.ascontiguousarray(words).reshape(g, 128, n, -1)
    if fmt == "e4m3":
        vals = words.view(ml_dtypes.float8_e4m3fn).astype(np.float64)
    else:
        nib = np.empty((g, 128, n, 4), np.uint8)
        nib[..., 0::2] = words & 0xF
        nib[..., 1::2] = words >> 4
        vals = E2M1[nib]
    vals = vals * np.repeat(np.exp2(scales.astype(np.float64) - 127.0), 8, axis=1)[..., None]
    return vals.transpose(0, 1, 3, 2).reshape(g * 512, n)


def silu(v):
    return v / (1.0 + np.exp(-v))


def bf(x):
    return np.asarray(x, np.float32).astype(ml_dtypes.bfloat16)


def planes(Y):
    r, m = Y.shape
    b = f64(bf(Y)).reshape(r // 32, 32, m)
    amax = np.abs(b).max(1)
    byte = np.clip(np.where(amax > 0, np.frexp(amax)[1] - 1 + 127 - 7, 1), 1, 254)
    codes = (b * np.exp2(127.0 - byte)[:, None, :]).reshape(r, m).astype(np.float32).astype(ml_dtypes.float8_e4m3fn).view(np.uint8)
    words = codes.reshape(r // 512, 128, 4, m).transpose(0, 1, 3, 2)
    return np.ascontiguousarray(words), np.ascontiguousarray(byte.astype(np.uint8).reshape(r // 512, 16, m))


K, T, J, N = 1024, 2048, 512, 512


def setup_inputs():
    n = np.random.standard_normal
    idx = np.random.permutation(T)[:J]
    fk = mx_kscale(K)
    wap = pack_weight(n((K, N)) * 1 / np.sqrt(K) * fk[:, None], "e2m1")
    wbp = pack_weight(n((K, N)) * 1 / np.sqrt(K) * fk[:, None], "e4m3")
    return {
        "xq": (n((K, T)) / fk[:, None]).astype(np.float32),
        "wa_words": wap[0],
        "wa_scales": wap[1],
        "wb_words": wbp[0],
        "wb_scales": wbp[1],
        "ga": (np.random.uniform(0.4, 1.2, (1, J))).astype(np.float32),
        "offs": striped(idx),
    }


def reference(xq, wa_words, wa_scales, wb_words, wb_scales, ga, offs):
    idx = unstriped(offs)
    wau = unpack_weight(wa_words, wa_scales, "e2m1")
    wbu = unpack_weight(wb_words, wb_scales, "e4m3")
    xqidxq = mxq(f64(xq)[:, idx], 0, "e4m3")
    p = wau.T @ xqidxq
    q = wbu.T @ xqidxq
    qs = np.pad(q, ((0, 0), (1, 0)))[:, :J]
    y = silu(p + f64(ga) * qs)
    words, scales = planes(y)
    return y, words, scales

@@ -1,0 +1,201 @@
+from contextlib import ExitStack
+
+import concourse.mybir as mybir
+from concourse.masks import make_identity
+
+K, T, J, N = 1024, 2048, 512, 512
+FLOPS = 2 * 2 * K * N * J
+
+F32 = mybir.dt.float32
+BF16 = mybir.dt.bfloat16
+I32 = mybir.dt.int32
+U32 = mybir.dt.uint32
+U16 = mybir.dt.uint16
+U8 = mybir.dt.uint8
+FP8X4 = mybir.dt.float8_e4m3fn_x4
+FP4X4 = mybir.dt.float4_e2m1fn_x4
+MULT = mybir.AluOpType.mult
+ADD = mybir.AluOpType.add
+SILU = mybir.ActivationFunctionType.Silu
+
+P = 128
+PACK = 4
+PASSES = K // (P * PACK)
+HALF = J // 2
+CHUNK = 128
+CHUNKS = J // CHUNK
+WB_ROW = 4
+LOAD_ORDER = [(0, 0), (0, 1), (0, 2), (1, 0), (1, 1), (0, 3), (1, 2), (1, 3)]
+
+
+def tile_list_expert_and_neighbour_pl_kernel(
+    tc, xq, wa_words, wa_scales, wb_words, wb_scales, ga, offs, out_0, out_1, out_2
+):
+    nc = tc.nc
+    with ExitStack() as ctx:
+        keep = ctx.enter_context(tc.tile_pool(name="keep", bufs=1))
+        psum = ctx.enter_context(tc.psum_pool(name="psum", bufs=1))
+
+        offsets = keep.tile([P, J // 16], U16, name="offsets")
+        nc.sync.dma_start(offsets[:], offs)
+        wb_raw = keep.tile([P, PASSES, N], I32, name="wb_raw")
+        wa_raw = keep.tile([P, PASSES, 2 * N], U8, name="wa_raw")
+        windows = {}
+        for step, (z, r) in enumerate(LOAD_ORDER):
+            if step == 2:
+                nc.sync.dma_start(out=wb_raw[:], in_=wb_words.rearrange("z p c r -> p z (c r)").bitcast(I32))
+                nc.sync.dma_start(out=wa_raw[:].bitcast(I32), in_=wa_words.rearrange("z p c -> p z c").bitcast(I32))
+            windows[z, r] = keep.tile([P, T], F32, name=f"window{z}{r}")
+            rows = xq[z * P * PACK : (z + 1) * P * PACK, :].rearrange("(p r) t -> p r t", r=PACK)
+            nc.sync.dma_start(out=windows[z, r][:], in_=rows[:, r, :])
+        ga_rows = keep.tile([P, PACK], F32, name="ga_rows")
+        nc.scalar.dma_start(out=ga_rows[:], in_=ga.rearrange("o (p f) -> (o p) f", f=PACK))
+
+        sc_raw = keep.tile([P, PASSES, N], U8, name="sc_raw")
+        nc.vector.memset(sc_raw[:].bitcast(I32), 0)
+        for q in range(4):
+            for row, src in ((0, wa_scales), (WB_ROW, wb_scales)):
+                nc.scalar.dma_start(
+                    out=sc_raw[32 * q + row : 32 * q + row + 4].bitcast(I32),
+                    in_=src[:, 4 * q : 4 * q + 4, :].rearrange("z r c -> r z c").bitcast(I32),
+                )
+
+        ident = keep.tile([P, P], F32, name="ident")
+        make_identity(nc, ident[:])
+        zeros = keep.tile([P, PACK], F32, name="zeros")
+        nc.vector.memset(zeros[:], 0.0)
+        msg = keep.tile([P, PACK, J + 8], F32, name="msg")
+        nc.scalar.activation(msg[:, :, 0], zeros[:], SILU)
+
+        ga_ps = psum.tile([P, PACK, P], F32, name="ga_ps", tag="bank_p3")
+        for f in range(PACK):
+            nc.tensor.transpose(ga_ps[:, f, :], ga_rows[:, f : f + 1].to_broadcast([P, P]), ident[:])
+        ga_all = keep.tile([P, J], F32, name="ga_all")
+        nc.scalar.copy(ga_all[:].rearrange("p (n f) -> p n f", f=PACK), ga_ps[:].rearrange("p f n -> p n f"))
+
+        wb = keep.tile([P, PASSES, N], I32, name="wb", align_bytes=64)
+        wa = keep.tile([P, PASSES, 2 * N], U8, name="wa", align_bytes=64)
+        sc = keep.tile([P, PASSES, N], U8, name="sc", align_bytes=64)
+
+        xb = {}
+        xc = {}
+        xs = {}
+        for z in range(PASSES):
+            for h in range(2):
+                xb[z, h] = keep.tile([P, HALF, PACK], BF16, name=f"xb{z}{h}", align_bytes=64)
+                xc[z, h] = keep.tile([P, HALF], U32, name=f"xc{z}{h}", align_bytes=64)
+                xs[z, h] = keep.tile([P, HALF], U8, name=f"xs{z}{h}", align_bytes=64)
+        pairs = [keep.tile([P, 2, J], BF16, name=f"pairs{z}") for z in range(PASSES)]
+        own = [psum.tile([P, PACK, CHUNK], F32, name=f"own{c}", tag=f"bank_p{c}") for c in range(CHUNKS)]
+        sent = [psum.tile([P, PACK, CHUNK], F32, name=f"sent{c}", tag=f"bank_q{c}") for c in range(CHUNKS)]
+
+        def gather(z, r, h):
+            entries = offsets[:, h * (HALF // 16) : (h + 1) * (HALF // 16)]
+            nc.vector.tensor_copy(xb[z, h][:, :, r], windows[z, r][:].indirect(entries))
+
+        def quantise(z, h):
+            nc.vector.quantize_mx(
+                out=xc[z, h][:].bitcast(FP8X4), scales=xs[z, h][:], in_=xb[z, h][:].rearrange("p j r -> p (j r)")
+            )
+
+        def products(z, h):
+            for is_own in (False, True):
+                for c in (2 * h, 2 * h + 1):
+                    cols = slice((c % 2) * CHUNK, (c % 2 + 1) * CHUNK)
+                    for s in range(PACK):
+                        if is_own:
+                            lhsT = wa[:, z, 2 * s * P : 2 * (s + 1) * P].bitcast(FP4X4)
+                            lhsT_scale = sc[:, z, s * P : (s + 1) * P]
+                        else:
+                            lhsT = wb[:, z, s * P : (s + 1) * P].bitcast(FP8X4)
+                            lhsT_scale = sc[WB_ROW:, z, s * P : (s + 1) * P]
+                        nc.tensor.matmul_mx(
+                            out=(own if is_own else sent)[c][:, s, :],
+                            lhsT=lhsT,
+                            lhsT_scale=lhsT_scale,
+                            rhs=xc[z, h][:, cols].bitcast(FP8X4),
+                            rhs_scale=xs[z, h][:, cols],
+                            start=(z == 0 and s == 0),
+                            stop=(z == PASSES - 1 and s == PACK - 1),
+                        )
+
+        for step, (z, r) in enumerate(LOAD_ORDER):
+            if step == 2:
+                for zz in range(PASSES):
+                    nc.vector.tensor_copy(
+                        out=wb[:, zz, :].rearrange("p (s a i) -> p a s i", s=PACK, i=4),
+                        in_=wb_raw[:, zz, :].rearrange("p (a i s) -> p a s i", s=PACK, i=4),
+                    )
+                    nc.vector.tensor_copy(
+                        out=wa[:, zz, :].bitcast(U16).rearrange("p (s a i) -> p a s i", s=PACK, i=8),
+                        in_=wa_raw[:, zz, :].bitcast(U16).rearrange("p (a i s) -> p a s i", s=PACK, i=8),
+                    )
+                    nc.vector.tensor_copy(
+                        out=sc[:, zz, :].rearrange("p (s a i) -> p a s i", s=PACK, i=16),
+                        in_=sc_raw[:, zz, :].rearrange("p (a i s) -> p a s i", s=PACK, i=16),
+                    )
+            if r < 2:
+                nc.vector.tensor_copy(pairs[z][:, r, :], windows[z, r][:].indirect(offsets[:]))
+                if r == 1:
+                    for h in range(2):
+                        nc.scalar.copy(
+                            xb[z, h][:, :, 0:2], pairs[z][:, :, h * HALF : (h + 1) * HALF].rearrange("p r j -> p j r")
+                        )
+                continue
+            for h in range(2):
+                gather(z, r, h)
+                if r == PACK - 1:
+                    quantise(z, h)
+                    products(z, h)
+
+        y_rows = out_0.rearrange("(p s) j -> p s j", s=PACK)
+        y_codes = keep.tile([P, J], U32, name="y_codes", align_bytes=64)
+        y_scales = keep.tile([P, J], U8, name="y_scales", align_bytes=64)
+        words_out = out_1[0].rearrange("p c r -> p (c r)").bitcast(I32)
+        yb = [keep.tile([P, CHUNK, PACK], BF16, name=f"yb{c}", align_bytes=64) for c in range(CHUNKS)]
+
+        def weigh(c):
+            first = c * CHUNK + 1
+            width = min(CHUNK, J - first)
+            nc.vector.tensor_tensor(
+                msg[:, :, first : first + width],
+                sent[c][:, :, 0:width],
+                ga_all[:, first : first + width].unsqueeze(1).to_broadcast([P, PACK, width]),
+                MULT,
+            )
+
+        def finish(c):
+            cols = slice(c * CHUNK, (c + 1) * CHUNK)
+            pre = keep.tile([P, PACK, CHUNK], F32, name=f"pre{c}")
+            nc.vector.tensor_tensor(pre[:], own[c][:], msg[:, :, cols], ADD)
+            y = keep.tile([P, PACK, CHUNK], F32, name=f"y{c}")
+            nc.scalar.activation(y[:], pre[:], SILU)
+            nc.sync.dma_start(out=y_rows[:, :, cols], in_=y[:])
+            ys.append(y)
+            if c < 2:
+                nc.scalar.copy(yb[c][:], y[:].rearrange("p s j -> p j s"))
+
+        def planes(c):
+            cols = slice(c * CHUNK, (c + 1) * CHUNK)
+            nc.vector.quantize_mx(
+                out=y_codes[:, cols].bitcast(FP8X4), scales=y_scales[:, cols], in_=yb[c][:].rearrange("p j s -> p (j s)")
+            )
+
+        ys = []
+        weigh(0)
+        for c in range(CHUNKS):
+            if c + 1 < CHUNKS:
+                weigh(c + 1)
+            finish(c)
+
+        planes(0)
+        planes(1)
+        nc.vector.tensor_copy(yb[2][:], ys[2][:].rearrange("p s j -> p j s"))
+        nc.sync.dma_start(out=words_out[:, 0:HALF], in_=y_codes[:, 0:HALF].bitcast(I32))
+        nc.vector.tensor_copy(yb[3][:], ys[3][:].rearrange("p s j -> p j s"))
+        planes(2)
+        planes(3)
+        nc.sync.dma_start(out=words_out[:, HALF:J], in_=y_codes[:, HALF:J].bitcast(I32))
+        for q in range(4):
+            queue = nc.sync if q < 2 else nc.scalar
+            queue.dma_start(out=out_2[0, 4 * q : 4 * q + 4, :].bitcast(I32), in_=y_scales[32 * q : 32 * q + 4, :].bitcast(I32))

@@ -64,8 +64,9 @@ def tile_list_expert_and_neighbour_pl_kernel(
         make_identity(nc, ident[:])
         zeros = keep.tile([P, PACK], F32, name="zeros")
         nc.vector.memset(zeros[:], 0.0)
-        msg = keep.tile([P, PACK, J + 8], F32, name="msg")
-        nc.scalar.activation(msg[:, :, 0], zeros[:], SILU)
+        msg = [keep.tile([P, PACK, CHUNK], F32, name=f"msg{c}") for c in range(CHUNKS)]
+        heard = {c: keep.tile([P, PACK, CHUNK], F32, name=f"heard{c}") for c in (0, 2)}
+        nc.scalar.activation(heard[0][:, :, 0], zeros[:], SILU)
 
         ga_ps = psum.tile([P, PACK, P], F32, name="ga_ps", tag="bank_p3")
         for f in range(PACK):
@@ -98,9 +99,10 @@ def tile_list_expert_and_neighbour_pl_kernel(
                 out=xc[z, h][:].bitcast(FP8X4), scales=xs[z, h][:], in_=xb[z, h][:].rearrange("p j r -> p (j r)")
             )
 
-        def products(z, h):
-            for is_own in (False, True):
-                for c in (2 * h, 2 * h + 1):
+        def products(z, chunks, is_own):
+            if True:
+                for c in chunks:
+                    h = c // 2
                     cols = slice((c % 2) * CHUNK, (c % 2 + 1) * CHUNK)
                     for s in range(PACK):
                         if is_own:
@@ -146,7 +148,9 @@ def tile_list_expert_and_neighbour_pl_kernel(
                 gather(z, r, h)
                 if r == PACK - 1:
                     quantise(z, h)
-                    products(z, h)
+                    products(z, (2 * h, 2 * h + 1), False)
+            if r == PACK - 1:
+                products(z, (1, 3, 0, 2), True)
 
         y_rows = out_0.rearrange("(p s) j -> p s j", s=PACK)
         y_codes = keep.tile([P, J], U32, name="y_codes", align_bytes=64)
@@ -154,26 +158,19 @@ def tile_list_expert_and_neighbour_pl_kernel(
         words_out = out_1[0].rearrange("p c r -> p (c r)").bitcast(I32)
         yb = [keep.tile([P, CHUNK, PACK], BF16, name=f"yb{c}", align_bytes=64) for c in range(CHUNKS)]
 
-        def weigh(c):
-            first = c * CHUNK + 1
-            width = min(CHUNK, J - first)
-            nc.vector.tensor_tensor(
-                msg[:, :, first : first + width],
-                sent[c][:, :, 0:width],
-                ga_all[:, first : first + width].unsqueeze(1).to_broadcast([P, PACK, width]),
-                MULT,
-            )
+
+        def ga_cols(first, width):
+            return ga_all[:, first : first + width].unsqueeze(1).to_broadcast([P, PACK, width])
 
         def finish(c):
             cols = slice(c * CHUNK, (c + 1) * CHUNK)
             pre = keep.tile([P, PACK, CHUNK], F32, name=f"pre{c}")
-            nc.vector.tensor_tensor(pre[:], own[c][:], msg[:, :, cols], ADD)
-            y = keep.tile([P, PACK, CHUNK], F32, name=f"y{c}")
-            nc.scalar.activation(y[:], pre[:], SILU)
-            nc.sync.dma_start(out=y_rows[:, :, cols], in_=y[:])
-            ys.append(y)
-            if c < 2:
-                nc.scalar.copy(yb[c][:], y[:].rearrange("p s j -> p j s"))
+            nc.vector.tensor_tensor(pre[:], own[c][:], msg[c][:], ADD)
+            nc.scalar.activation(ys[c][:], pre[:], SILU)
+            nc.sync.dma_start(out=y_rows[:, :, cols], in_=ys[c][:])
+
+        def round_y(engine_copy, c):
+            engine_copy(yb[c][:], ys[c][:].rearrange("p s j -> p j s"))
 
         def planes(c):
             cols = slice(c * CHUNK, (c + 1) * CHUNK)
@@ -181,21 +178,27 @@ def tile_list_expert_and_neighbour_pl_kernel(
                 out=y_codes[:, cols].bitcast(FP8X4), scales=y_scales[:, cols], in_=yb[c][:].rearrange("p j s -> p (j s)")
             )
 
-        ys = []
-        weigh(0)
-        for c in range(CHUNKS):
-            if c + 1 < CHUNKS:
-                weigh(c + 1)
+        ys = [keep.tile([P, PACK, CHUNK], F32, name=f"y{c}") for c in range(CHUNKS)]
+        last = CHUNK - 1
+        for c in (0, 2):
+            nc.scalar.copy(heard[c][:, :, 1:CHUNK], sent[c][:, :, 0:last])
+            nc.vector.tensor_tensor(msg[c + 1][:, :, 1:CHUNK], sent[c + 1][:, :, 0:last], ga_cols((c + 1) * CHUNK + 1, last), MULT)
+            if c > 0:
+                nc.scalar.copy(heard[c][:, :, 0:1], sent[c - 1][:, :, last:CHUNK])
+            nc.gpsimd.tensor_tensor(msg[c][:], heard[c][:], ga_cols(c * CHUNK, CHUNK), MULT)
+            nc.vector.tensor_tensor(msg[c + 1][:, :, 0:1], sent[c][:, :, last:CHUNK], ga_cols((c + 1) * CHUNK, 1), MULT)
+        for c in (1, 3, 0, 2):
             finish(c)
-
-        planes(0)
+        round_y(nc.vector.tensor_copy, 1)
+        round_y(nc.vector.tensor_copy, 3)
+        round_y(nc.scalar.copy, 0)
         planes(1)
-        nc.vector.tensor_copy(yb[2][:], ys[2][:].rearrange("p s j -> p j s"))
-        nc.sync.dma_start(out=words_out[:, 0:HALF], in_=y_codes[:, 0:HALF].bitcast(I32))
-        nc.vector.tensor_copy(yb[3][:], ys[3][:].rearrange("p s j -> p j s"))
-        planes(2)
+        round_y(nc.vector.tensor_copy, 2)
         planes(3)
+        planes(2)
         nc.sync.dma_start(out=words_out[:, HALF:J], in_=y_codes[:, HALF:J].bitcast(I32))
+        planes(0)
+        nc.sync.dma_start(out=words_out[:, 0:HALF], in_=y_codes[:, 0:HALF].bitcast(I32))
         for q in range(4):
             queue = nc.sync if q < 2 else nc.scalar
             queue.dma_start(out=out_2[0, 4 * q : 4 * q + 4, :].bitcast(I32), in_=y_scales[32 * q : 32 * q + 4, :].bitcast(I32))

@@ -39,15 +39,16 @@ def tile_list_expert_and_neighbour_pl_kernel(
         offsets = keep.tile([P, J // 16], U16, name="offsets")
         nc.sync.dma_start(offsets[:], offs)
         wb_raw = keep.tile([P, PASSES, N], I32, name="wb_raw")
-        wa_raw = keep.tile([P, PASSES, 2 * N], U8, name="wa_raw")
+        wa_raw = [keep.tile([P, 2 * N], U8, name=f"wa_raw{z}") for z in range(PASSES)]
         windows = {}
         for step, (z, r) in enumerate(LOAD_ORDER):
             if step == 2:
                 nc.sync.dma_start(out=wb_raw[:], in_=wb_words.rearrange("z p c r -> p z (c r)").bitcast(I32))
-                nc.sync.dma_start(out=wa_raw[:].bitcast(I32), in_=wa_words.rearrange("z p c -> p z c").bitcast(I32))
+                nc.sync.dma_start(out=wa_raw[0][:].bitcast(I32), in_=wa_words[0].bitcast(I32))
             windows[z, r] = keep.tile([P, T], F32, name=f"window{z}{r}")
             rows = xq[z * P * PACK : (z + 1) * P * PACK, :].rearrange("(p r) t -> p r t", r=PACK)
             nc.sync.dma_start(out=windows[z, r][:], in_=rows[:, r, :])
+        nc.sync.dma_start(out=wa_raw[1][:].bitcast(I32), in_=wa_words[1].bitcast(I32))
         ga_rows = keep.tile([P, PACK], F32, name="ga_rows")
         nc.scalar.dma_start(out=ga_rows[:], in_=ga.rearrange("o (p f) -> (o p) f", f=PACK))
 
@@ -75,7 +76,14 @@ def tile_list_expert_and_neighbour_pl_kernel(
         nc.scalar.copy(ga_all[:].rearrange("p (n f) -> p n f", f=PACK), ga_ps[:].rearrange("p f n -> p n f"))
 
         wb = keep.tile([P, PASSES, N], I32, name="wb", align_bytes=64)
-        wa = keep.tile([P, PASSES, 2 * N], U8, name="wa", align_bytes=64)
+        wa = [keep.tile([P, 2 * N], U8, name=f"wa{z}", align_bytes=64) for z in range(PASSES)]
+
+        def deal_wa(z):
+            nc.vector.tensor_copy(
+                out=wa[z][:].bitcast(U16).rearrange("p (s a i) -> p a s i", s=PACK, i=8),
+                in_=wa_raw[z][:].bitcast(U16).rearrange("p (a i s) -> p a s i", s=PACK, i=8),
+            )
+
         sc = keep.tile([P, PASSES, N], U8, name="sc", align_bytes=64)
 
         xb = {}
@@ -95,9 +103,13 @@ def tile_list_expert_and_neighbour_pl_kernel(
             nc.vector.tensor_copy(xb[z, h][:, :, r], windows[z, r][:].indirect(entries))
 
         def quantise(z, h):
-            nc.vector.quantize_mx(
-                out=xc[z, h][:].bitcast(FP8X4), scales=xs[z, h][:], in_=xb[z, h][:].rearrange("p j r -> p (j r)")
-            )
+            for u in range(2):
+                cols = slice(u * CHUNK, (u + 1) * CHUNK)
+                nc.vector.quantize_mx(
+                    out=xc[z, h][:, cols].bitcast(FP8X4),
+                    scales=xs[z, h][:, cols],
+                    in_=xb[z, h][:, cols, :].rearrange("p j r -> p (j r)"),
+                )
 
         def products(z, chunks, is_own):
             if True:
@@ -106,7 +118,7 @@ def tile_list_expert_and_neighbour_pl_kernel(
                     cols = slice((c % 2) * CHUNK, (c % 2 + 1) * CHUNK)
                     for s in range(PACK):
                         if is_own:
-                            lhsT = wa[:, z, 2 * s * P : 2 * (s + 1) * P].bitcast(FP4X4)
+                            lhsT = wa[z][:, 2 * s * P : 2 * (s + 1) * P].bitcast(FP4X4)
                             lhsT_scale = sc[:, z, s * P : (s + 1) * P]
                         else:
                             lhsT = wb[:, z, s * P : (s + 1) * P].bitcast(FP8X4)
@@ -128,10 +140,8 @@ def tile_list_expert_and_neighbour_pl_kernel(
                         out=wb[:, zz, :].rearrange("p (s a i) -> p a s i", s=PACK, i=4),
                         in_=wb_raw[:, zz, :].rearrange("p (a i s) -> p a s i", s=PACK, i=4),
                     )
-                    nc.vector.tensor_copy(
-                        out=wa[:, zz, :].bitcast(U16).rearrange("p (s a i) -> p a s i", s=PACK, i=8),
-                        in_=wa_raw[:, zz, :].bitcast(U16).rearrange("p (a i s) -> p a s i", s=PACK, i=8),
-                    )
+                    if zz == 0:
+                        deal_wa(0)
                     nc.vector.tensor_copy(
                         out=sc[:, zz, :].rearrange("p (s a i) -> p a s i", s=PACK, i=16),
                         in_=sc_raw[:, zz, :].rearrange("p (a i s) -> p a s i", s=PACK, i=16),
@@ -150,6 +160,8 @@ def tile_list_expert_and_neighbour_pl_kernel(
                     quantise(z, h)
                     products(z, (2 * h, 2 * h + 1), False)
             if r == PACK - 1:
+                if z == 1:
+                    deal_wa(1)
                 products(z, (1, 3, 0, 2), True)
 
         y_rows = out_0.rearrange("(p s) j -> p s j", s=PACK)

from contextlib import ExitStack

import concourse.mybir as mybir
from concourse.masks import make_identity

K, T, J, N = 1024, 2048, 512, 512
FLOPS = 2 * 2 * K * N * J

F32 = mybir.dt.float32
BF16 = mybir.dt.bfloat16
I32 = mybir.dt.int32
U32 = mybir.dt.uint32
U16 = mybir.dt.uint16
U8 = mybir.dt.uint8
FP8X4 = mybir.dt.float8_e4m3fn_x4
FP4X4 = mybir.dt.float4_e2m1fn_x4
MULT = mybir.AluOpType.mult
ADD = mybir.AluOpType.add
SILU = mybir.ActivationFunctionType.Silu

P = 128
PACK = 4
PASSES = K // (P * PACK)
HALF = J // 2
CHUNK = 128
CHUNKS = J // CHUNK
WB_ROW = 4
LOAD_ORDER = [(0, 0), (0, 1), (0, 2), (1, 0), (1, 1), (0, 3), (1, 2), (1, 3)]


def tile_list_expert_and_neighbour_pl_kernel(
    tc, xq, wa_words, wa_scales, wb_words, wb_scales, ga, offs, out_0, out_1, out_2
):
    nc = tc.nc
    with ExitStack() as ctx:
        keep = ctx.enter_context(tc.tile_pool(name="keep", bufs=1))
        psum = ctx.enter_context(tc.psum_pool(name="psum", bufs=1))

        offsets = keep.tile([P, J // 16], U16, name="offsets")
        nc.sync.dma_start(offsets[:], offs)
        wb_raw = keep.tile([P, PASSES, N], I32, name="wb_raw")
        wa_raw = [keep.tile([P, 2 * N], U8, name=f"wa_raw{z}") for z in range(PASSES)]
        windows = {}
        for step, (z, r) in enumerate(LOAD_ORDER):
            if step == 2:
                nc.sync.dma_start(out=wb_raw[:], in_=wb_words.rearrange("z p c r -> p z (c r)").bitcast(I32))
                nc.sync.dma_start(out=wa_raw[0][:].bitcast(I32), in_=wa_words[0].bitcast(I32))
            windows[z, r] = keep.tile([P, T], F32, name=f"window{z}{r}")
            rows = xq[z * P * PACK : (z + 1) * P * PACK, :].rearrange("(p r) t -> p r t", r=PACK)
            nc.sync.dma_start(out=windows[z, r][:], in_=rows[:, r, :])
        nc.sync.dma_start(out=wa_raw[1][:].bitcast(I32), in_=wa_words[1].bitcast(I32))
        ga_rows = keep.tile([P, PACK], F32, name="ga_rows")
        nc.scalar.dma_start(out=ga_rows[:], in_=ga.rearrange("o (p f) -> (o p) f", f=PACK))

        sc_raw = keep.tile([P, PASSES, N], U8, name="sc_raw")
        nc.vector.memset(sc_raw[:].bitcast(I32), 0)
        for q in range(4):
            for row, src in ((0, wa_scales), (WB_ROW, wb_scales)):
                nc.scalar.dma_start(
                    out=sc_raw[32 * q + row : 32 * q + row + 4].bitcast(I32),
                    in_=src[:, 4 * q : 4 * q + 4, :].rearrange("z r c -> r z c").bitcast(I32),
                )

        ident = keep.tile([P, P], F32, name="ident")
        make_identity(nc, ident[:])
        zeros = keep.tile([P, PACK], F32, name="zeros")
        nc.vector.memset(zeros[:], 0.0)
        msg = [keep.tile([P, PACK, CHUNK], F32, name=f"msg{c}") for c in range(CHUNKS)]
        heard = {c: keep.tile([P, PACK, CHUNK], F32, name=f"heard{c}") for c in (0, 2)}
        nc.scalar.activation(heard[0][:, :, 0], zeros[:], SILU)

        ga_ps = psum.tile([P, PACK, P], F32, name="ga_ps", tag="bank_p3")
        for f in range(PACK):
            nc.tensor.transpose(ga_ps[:, f, :], ga_rows[:, f : f + 1].to_broadcast([P, P]), ident[:])
        ga_all = keep.tile([P, J], F32, name="ga_all")
        nc.scalar.copy(ga_all[:].rearrange("p (n f) -> p n f", f=PACK), ga_ps[:].rearrange("p f n -> p n f"))

        wb = keep.tile([P, PASSES, N], I32, name="wb", align_bytes=64)
        wa = [keep.tile([P, 2 * N], U8, name=f"wa{z}", align_bytes=64) for z in range(PASSES)]

        def deal_wa(z):
            nc.vector.tensor_copy(
                out=wa[z][:].bitcast(U16).rearrange("p (s a i) -> p a s i", s=PACK, i=8),
                in_=wa_raw[z][:].bitcast(U16).rearrange("p (a i s) -> p a s i", s=PACK, i=8),
            )

        sc = keep.tile([P, PASSES, N], U8, name="sc", align_bytes=64)

        xb = {}
        xc = {}
        xs = {}
        for z in range(PASSES):
            for h in range(2):
                xb[z, h] = keep.tile([P, HALF, PACK], BF16, name=f"xb{z}{h}", align_bytes=64)
                xc[z, h] = keep.tile([P, HALF], U32, name=f"xc{z}{h}", align_bytes=64)
                xs[z, h] = keep.tile([P, HALF], U8, name=f"xs{z}{h}", align_bytes=64)
        pairs = [keep.tile([P, 2, J], BF16, name=f"pairs{z}") for z in range(PASSES)]
        own = [psum.tile([P, PACK, CHUNK], F32, name=f"own{c}", tag=f"bank_p{c}") for c in range(CHUNKS)]
        sent = [psum.tile([P, PACK, CHUNK], F32, name=f"sent{c}", tag=f"bank_q{c}") for c in range(CHUNKS)]

        def gather(z, r, h):
            entries = offsets[:, h * (HALF // 16) : (h + 1) * (HALF // 16)]
            nc.vector.tensor_copy(xb[z, h][:, :, r], windows[z, r][:].indirect(entries))

        def quantise(z, h):
            for u in range(2):
                cols = slice(u * CHUNK, (u + 1) * CHUNK)
                nc.vector.quantize_mx(
                    out=xc[z, h][:, cols].bitcast(FP8X4),
                    scales=xs[z, h][:, cols],
                    in_=xb[z, h][:, cols, :].rearrange("p j r -> p (j r)"),
                )

        def products(z, chunks, is_own):
            if True:
                for c in chunks:
                    h = c // 2
                    cols = slice((c % 2) * CHUNK, (c % 2 + 1) * CHUNK)
                    for s in range(PACK):
                        if is_own:
                            lhsT = wa[z][:, 2 * s * P : 2 * (s + 1) * P].bitcast(FP4X4)
                            lhsT_scale = sc[:, z, s * P : (s + 1) * P]
                        else:
                            lhsT = wb[:, z, s * P : (s + 1) * P].bitcast(FP8X4)
                            lhsT_scale = sc[WB_ROW:, z, s * P : (s + 1) * P]
                        nc.tensor.matmul_mx(
                            out=(own if is_own else sent)[c][:, s, :],
                            lhsT=lhsT,
                            lhsT_scale=lhsT_scale,
                            rhs=xc[z, h][:, cols].bitcast(FP8X4),
                            rhs_scale=xs[z, h][:, cols],
                            start=(z == 0 and s == 0),
                            stop=(z == PASSES - 1 and s == PACK - 1),
                        )

        for step, (z, r) in enumerate(LOAD_ORDER):
            if step == 2:
                for zz in range(PASSES):
                    nc.vector.tensor_copy(
                        out=wb[:, zz, :].rearrange("p (s a i) -> p a s i", s=PACK, i=4),
                        in_=wb_raw[:, zz, :].rearrange("p (a i s) -> p a s i", s=PACK, i=4),
                    )
                    if zz == 0:
                        deal_wa(0)
                    nc.vector.tensor_copy(
                        out=sc[:, zz, :].rearrange("p (s a i) -> p a s i", s=PACK, i=16),
                        in_=sc_raw[:, zz, :].rearrange("p (a i s) -> p a s i", s=PACK, i=16),
                    )
            if r < 2:
                nc.vector.tensor_copy(pairs[z][:, r, :], windows[z, r][:].indirect(offsets[:]))
                if r == 1:
                    for h in range(2):
                        nc.scalar.copy(
                            xb[z, h][:, :, 0:2], pairs[z][:, :, h * HALF : (h + 1) * HALF].rearrange("p r j -> p j r")
                        )
                continue
            for h in range(2):
                gather(z, r, h)
                if r == PACK - 1:
                    quantise(z, h)
                    products(z, (2 * h, 2 * h + 1), False)
            if r == PACK - 1:
                if z == 1:
                    deal_wa(1)
                products(z, (1, 3, 0, 2), True)

        y_rows = out_0.rearrange("(p s) j -> p s j", s=PACK)
        y_codes = keep.tile([P, J], U32, name="y_codes", align_bytes=64)
        y_scales = keep.tile([P, J], U8, name="y_scales", align_bytes=64)
        words_out = out_1[0].rearrange("p c r -> p (c r)").bitcast(I32)
        yb = [keep.tile([P, CHUNK, PACK], BF16, name=f"yb{c}", align_bytes=64) for c in range(CHUNKS)]


        def ga_cols(first, width):
            return ga_all[:, first : first + width].unsqueeze(1).to_broadcast([P, PACK, width])

        def finish(c):
            cols = slice(c * CHUNK, (c + 1) * CHUNK)
            pre = keep.tile([P, PACK, CHUNK], F32, name=f"pre{c}")
            nc.vector.tensor_tensor(pre[:], own[c][:], msg[c][:], ADD)
            nc.scalar.activation(ys[c][:], pre[:], SILU)
            nc.sync.dma_start(out=y_rows[:, :, cols], in_=ys[c][:])

        def round_y(engine_copy, c):
            engine_copy(yb[c][:], ys[c][:].rearrange("p s j -> p j s"))

        def planes(c):
            cols = slice(c * CHUNK, (c + 1) * CHUNK)
            nc.vector.quantize_mx(
                out=y_codes[:, cols].bitcast(FP8X4), scales=y_scales[:, cols], in_=yb[c][:].rearrange("p j s -> p (j s)")
            )

        ys = [keep.tile([P, PACK, CHUNK], F32, name=f"y{c}") for c in range(CHUNKS)]
        last = CHUNK - 1
        for c in (0, 2):
            nc.scalar.copy(heard[c][:, :, 1:CHUNK], sent[c][:, :, 0:last])
            nc.vector.tensor_tensor(msg[c + 1][:, :, 1:CHUNK], sent[c + 1][:, :, 0:last], ga_cols((c + 1) * CHUNK + 1, last), MULT)
            if c > 0:
                nc.scalar.copy(heard[c][:, :, 0:1], sent[c - 1][:, :, last:CHUNK])
            nc.gpsimd.tensor_tensor(msg[c][:], heard[c][:], ga_cols(c * CHUNK, CHUNK), MULT)
            nc.vector.tensor_tensor(msg[c + 1][:, :, 0:1], sent[c][:, :, last:CHUNK], ga_cols((c + 1) * CHUNK, 1), MULT)
        for c in (1, 3, 0, 2):
            finish(c)
        round_y(nc.vector.tensor_copy, 1)
        round_y(nc.vector.tensor_copy, 3)
        round_y(nc.scalar.copy, 0)
        planes(1)
        round_y(nc.vector.tensor_copy, 2)
        planes(3)
        planes(2)
        nc.sync.dma_start(out=words_out[:, HALF:J], in_=y_codes[:, HALF:J].bitcast(I32))
        planes(0)
        nc.sync.dma_start(out=words_out[:, 0:HALF], in_=y_codes[:, 0:HALF].bitcast(I32))
        for q in range(4):
            queue = nc.sync if q < 2 else nc.scalar
            queue.dma_start(out=out_2[0, 4 * q : 4 * q + 4, :].bitcast(I32), in_=y_scales[32 * q : 32 * q + 4, :].bitcast(I32))
